import numpy as np
import ml_dtypes


def mxq(x, axis, fmt="e4m3"):
    dtype, down = {"e4m3": (ml_dtypes.float8_e4m3fn, 7), "e5m2": (ml_dtypes.float8_e5m2, 14)}[fmt]
    v = np.moveaxis(np.asarray(x, np.float32).astype(ml_dtypes.bfloat16).astype(np.float64), axis, -1)
    blocks = v.reshape(v.shape[:-1] + (-1, 32))
    amax = np.abs(blocks).max(-1, keepdims=True)
    byte = np.maximum(np.where(amax > 0, np.frexp(amax)[1] - 1 + 127, 0) - down, 1)
    scale = np.exp2(byte - 127.0)
    codes = (blocks / scale).astype(np.float32).astype(dtype).astype(np.float64)
    return np.moveaxis((codes * scale).reshape(v.shape), -1, axis)


WIDE = False


def mx_kscale(k):
    if not WIDE:
        return np.ones(k)
    levels = np.array([30, -30])
    if k % 512:
        return np.exp2(np.random.permutation(np.resize(levels, k // 32))).repeat(32)
    a = np.empty((k // 512, 16))
    for p in range(k // 512):
        a[p, :8] = np.random.permutation(np.resize(levels, 8))
        for g in range(8):
            far = levels[np.abs(levels - a[p, g]) >= 10]
            a[p, g + 8] = far[np.random.randint(len(far))]
    return np.exp2(a.ravel()).repeat(32)


def f64(x):
    return np.asarray(x).astype(np.float64)


def striped(idx):
    return np.tile(idx.reshape(-1, 16).T, (8, 1)).astype(np.uint16)


def unstriped(offs):
    return offs[:16].T.reshape(-1).astype(np.int64)


E2M1 = np.array([0.0, 0.5, 1.0, 1.5, 2.0, 3.0, 4.0, 6.0, -0.0, -0.5, -1.0, -1.5, -2.0, -3.0, -4.0, -6.0])


def pack_weight(w, fmt):
    k, n = w.shape
    w = f64(np.asarray(w, np.float32).astype(ml_dtypes.bfloat16)).reshape(k // 32, 32, n)
    amax = np.abs(w).max(1)
    if fmt == "e4m3":
        byte = np.frexp(amax)[1] - 1 + 127 - 7
    else:
        mant, ex = np.frexp(amax / 6.0)
        byte = np.where(mant > 0.5, ex, ex - 1) + 127
    byte = np.clip(np.where(amax > 0, byte, 1), 1, 254)
    scaled = (w * np.exp2(127.0 - byte)[:, None, :]).reshape(k, n).astype(np.float32)
    by_word = np.ascontiguousarray(scaled.reshape(k // 512, 128, 4, n).transpose(0, 1, 3, 2))
    if fmt == "e4m3":
        words = by_word.astype(ml_dtypes.float8_e4m3fn).view(np.uint8)
    else:
        c = by_word.astype(ml_dtypes.float4_e2m1fn).view(np.uint8) & 0xF
        words = (c[..., 0::2] | (c[..., 1::2] << 4)).reshape(k // 512, 128, 2 * n)
    return np.ascontiguousarray(words), np.ascontiguousarray(byte.astype(np.uint8).reshape(k // 512, 16, n))


def unpack_weight(words, scales, fmt):
    g, _, n = scales.shape
    words = np.ascontiguousarray(words).reshape(g, 128, n, -1)
    if fmt == "e4m3":
        vals = words.view(ml_dtypes.float8_e4m3fn).astype(np.float64)
    else:
        nib = np.empty((g, 128, n, 4), np.uint8)
        nib[..., 0::2] = words & 0xF
        nib[..., 1::2] = words >> 4
        vals = E2M1[nib]
    vals = vals * np.repeat(np.exp2(scales.astype(np.float64) - 127.0), 8, axis=1)[..., None]
    return vals.transpose(0, 1, 3, 2).reshape(g * 512, n)


def d_relu2(v):
    return 2.0 * np.maximum(v, 0.0)


K, T, E, C, H, N = 256, 1024, 2, 512, 1024, 1024


def by_expert(wq, xq):
    return np.concatenate([wq[e].T @ xq[:, e * C:(e + 1) * C] for e in range(E)], axis=1)


def setup_inputs():
    n = np.random.standard_normal
    s = mx_kscale(N)[:, None]
    u = mx_kscale(H)
    w2 = [pack_weight(m, "e2m1") for m in n((E, N, H)) / np.sqrt(N) / s[None] * u[None, None, :]]
    w1 = [pack_weight(m, "e2m1") for m in n((E, H, K)) / np.sqrt(H) / u[None, :, None]]
    return {
        "dyT": (n((N, T)) * s).astype(np.float32),
        "a": n((H, E * C)).astype(np.float32),
        "w2_words": np.stack([m[0] for m in w2]),
        "w2_scales": np.stack([m[1] for m in w2]),
        "w1_words": np.stack([m[0] for m in w1]),
        "w1_scales": np.stack([m[1] for m in w1]),
        "gate": np.tile(np.random.uniform(0.2, 1.0, E * C), (N, 1)).astype(np.float32),
        "offs": striped(np.random.permutation(T)[:E * C]),
    }


def reference(dyT, a, w2_words, w2_scales, w1_words, w1_scales, gate, offs):
    idx = unstriped(offs)
    w2 = np.stack([unpack_weight(w2_words[e], w2_scales[e], "e2m1") for e in range(E)])
    w1 = np.stack([unpack_weight(w1_words[e], w1_scales[e], "e2m1") for e in range(E)])
    gq = mxq(f64(gate) * f64(dyT)[:, idx], 0, "e5m2")
    dh = by_expert(w2, gq)
    da = dh * d_relu2(f64(a))
    dx = by_expert(w1, mxq(da, 0, "e5m2"))
    out = np.zeros((K, T))
    out[:, idx] = dx
    return out

@@ -1,0 +1,188 @@
+from contextlib import ExitStack
+
+import concourse.mybir as mybir
+
+K, T, E, C, H, N = 256, 1024, 2, 512, 1024, 1024
+P = 128
+PACK = 4
+PASS = P * PACK
+FLOPS = 2 * E * C * H * (N + K)
+BYTES = 4 * (N * T + H * E * C + K * T + E * C) + E * N * H // 2 + E * H * K // 2 + E * N * H // 32 + E * H * K // 32 + 2 * E * C
+
+F32 = mybir.dt.float32
+BF16 = mybir.dt.bfloat16
+I32 = mybir.dt.int32
+U32 = mybir.dt.uint32
+U16 = mybir.dt.uint16
+U8 = mybir.dt.uint8
+E5M2 = mybir.dt.float8_e5m2_x4
+E2M1 = mybir.dt.float4_e2m1fn_x4
+ALU = mybir.AluOpType
+COPY = mybir.ActivationFunctionType.Copy
+
+
+def tile_moe_bdx_mlp_relu2_kernel(
+    tc, dyT, a, w2_words, w2_scales, w1_words, w1_scales, gate, offs, out
+):
+    nc = tc.nc
+    SN, SI, KT = N // PASS, H // PASS, K // P
+    last = E - 1
+
+    def cuts(e, s):
+        if e == last and s == 1:
+            return [(0, C // 2), (C // 2, C)]
+        return [(0, C)]
+
+    with ExitStack() as ctx:
+        held = ctx.enter_context(tc.tile_pool(name="held", bufs=1))
+        psum = ctx.enter_context(tc.psum_pool(name="psum", bufs=1))
+
+        offsets = held.tile([P, E * C // 16], U16, name="offsets")
+        dy_t = [[held.tile([P, T], F32, name=f"dy{s}{t}") for t in range(PACK)] for s in range(SN)]
+        gate_t = [held.tile([P, C], F32, name=f"gate{e}") for e in range(E)]
+        a_t = [[held.tile([P, PACK, C], F32, name=f"a{e}{s}") for s in range(SI)] for e in range(E)]
+        w2_raw = [held.tile([P, SN, 2 * H], U8, name=f"w2r{e}", align_bytes=64) for e in range(E)]
+        w2_p = [held.tile([P, SN, 2 * H], U8, name=f"w2p{e}", align_bytes=64) for e in range(E)]
+        w2s_raw = held.tile([P, E * SN, H], U8, name="w2sr", align_bytes=64)
+        w2s_p = [held.tile([P, SN, H], U8, name=f"w2sp{e}", align_bytes=64) for e in range(E)]
+        w1_t = held.tile([P, E * SI, 2 * K], U8, name="w1t", align_bytes=64)
+        w1s_t = held.tile([P, E * SI, K], U8, name="w1s", align_bytes=64)
+        win = [held.tile([P, T], F32, name=f"win{k}") for k in range(KT)]
+
+        dy_v = dyT.rearrange("(s p t) c -> s t p c", p=P, t=PACK)
+        a_v = a.rearrange("(s p t) (e c) -> e s p t c", p=P, t=PACK, e=E)
+        w2_v = w2_words.bitcast(I32)
+        w2s_v = w2_scales.bitcast(I32).rearrange("e s f i -> f (e s) i")
+        w1_v = w1_words.bitcast(I32).rearrange("e s p b -> p (e s) b")
+        w1s_v = w1_scales.bitcast(I32).rearrange("e s f i -> f (e s) i")
+
+        nc.sync.dma_start(offsets[:], offs)
+        nc.vector.memset(w2s_raw[:].bitcast(I32), 0)
+        nc.vector.memset(w1s_t[:].bitcast(I32), 0)
+
+        def load_w2(e):
+            for s in range(SN):
+                nc.sync.dma_start(w2_raw[e][:, s, :].bitcast(I32), w2_v[e, s])
+
+        load_w2(0)
+        nc.sync.dma_start(gate_t[0][:], gate[0:P, 0:C])
+        for t in range(PACK):
+            nc.sync.dma_start(dy_t[0][t][:], dy_v[0, t])
+        for q in range(4):
+            nc.sync.dma_start(w2s_raw[32 * q : 32 * q + 4, :, :].bitcast(I32), w2s_v[4 * q : 4 * q + 4])
+        for t in range(PACK):
+            nc.sync.dma_start(dy_t[1][t][:], dy_v[1, t])
+        nc.sync.dma_start(w1_t[:].bitcast(I32), w1_v)
+        for q in range(4):
+            nc.sync.dma_start(w1s_t[32 * q : 32 * q + 4, :, :].bitcast(I32), w1s_v[4 * q : 4 * q + 4])
+        for s in range(SI):
+            nc.sync.dma_start(a_t[0][s][:], a_v[0, s])
+        nc.sync.dma_start(gate_t[1][:], gate[0:P, C : 2 * C])
+        load_w2(1)
+        for s in range(SI):
+            nc.sync.dma_start(a_t[1][s][:], a_v[1, s])
+
+        def permute_w2_words(e):
+            for s in range(SN):
+                nc.vector.tensor_copy(
+                    out=w2_p[e][:, s, :].bitcast(U16).rearrange("p (s t m) -> p s t m", s=SI, t=PACK),
+                    in_=w2_raw[e][:, s, :].bitcast(U16).rearrange("p (s m t) -> p s t m", s=SI, t=PACK),
+                )
+
+        def permute_w2_scales(e):
+            nc.vector.tensor_copy(
+                out=w2s_p[e][:].rearrange("p n (s t m) -> p (n s) t m", s=SI, t=PACK),
+                in_=w2s_raw[:, e * SN : (e + 1) * SN, :].rearrange("p n (s m t) -> p (n s) t m", s=SI, t=PACK),
+            )
+
+        g_codes = {}
+        g_scales = {}
+
+        def gather_and_quantize(e, s):
+            g = held.tile([P, PACK, C], F32, name=f"g{e}{s}")
+            gi = held.tile([P, C, PACK], BF16, name=f"gi{e}{s}", align_bytes=64)
+            codes = held.tile([P, C], U32, name=f"gc{e}{s}", align_bytes=64)
+            scales = held.tile([P, C], U8, name=f"gs{e}{s}", align_bytes=64)
+            for lo, hi in cuts(e, s):
+                o = offsets[:, (e * C + lo) // 16 : (e * C + hi) // 16]
+                for t in range(PACK):
+                    nc.vector.tensor_tensor(g[:, t, lo:hi], dy_t[s][t][:].indirect(o), gate_t[e][:, lo:hi], ALU.mult)
+                nc.scalar.copy(out=gi[:, lo:hi, :], in_=g[:, :, lo:hi].rearrange("p t c -> p c t"))
+                nc.vector.quantize_mx(
+                    out=codes[:, lo:hi].bitcast(E5M2), scales=scales[:, lo:hi], in_=gi[:, lo:hi, :].rearrange("p c t -> p (c t)")
+                )
+            g_codes[e, s] = codes
+            g_scales[e, s] = scales
+
+        dx = {}
+
+        def layers(e):
+            da_codes = []
+            da_scales = []
+            for si in range(SI):
+                da = held.tile([P, PACK, C], BF16, name=f"da{e}{si}")
+                dai = held.tile([P, C, PACK], BF16, name=f"dai{e}{si}", align_bytes=64)
+                codes = held.tile([P, C], U32, name=f"dc{e}{si}", align_bytes=64)
+                scales = held.tile([P, C], U8, name=f"ds{e}{si}", align_bytes=64)
+                banks = []
+                for t in range(PACK):
+                    m0 = (si * PACK + t) * P
+                    dh = psum.tile([P, C], F32, name=f"dh{(si * PACK + t) % 6}")
+                    for s in range(SN):
+                        nc.tensor.matmul_mx(
+                            out=dh[:],
+                            lhsT=w2_p[e][:, s, 2 * m0 : 2 * (m0 + P)].bitcast(E2M1),
+                            lhsT_scale=w2s_p[e][:, s, m0 : m0 + P],
+                            rhs=g_codes[e, s][:].bitcast(E5M2),
+                            rhs_scale=g_scales[e, s][:],
+                            start=(s == 0),
+                            stop=(s == SN - 1),
+                        )
+                    banks.append(dh)
+                for lo, hi in cuts(e, si):
+                    for t in range(PACK):
+                        nc.vector.scalar_tensor_tensor(
+                            out=da[:, t, lo:hi], in0=a_t[e][si][:, t, lo:hi], scalar=0.0, in1=banks[t][:, lo:hi], op0=ALU.max, op1=ALU.mult
+                        )
+                    nc.scalar.copy(out=dai[:, lo:hi, :], in_=da[:, :, lo:hi].rearrange("p t c -> p c t"))
+                    nc.vector.quantize_mx(
+                        out=codes[:, lo:hi].bitcast(E5M2), scales=scales[:, lo:hi], in_=dai[:, lo:hi, :].rearrange("p c t -> p (c t)")
+                    )
+                da_codes.append(codes)
+                da_scales.append(scales)
+            for k in range(KT):
+                acc = psum.tile([P, C], F32, name=f"acc{k}")
+                for si in range(SI):
+                    nc.tensor.matmul_mx(
+                        out=acc[:],
+                        lhsT=w1_t[:, e * SI + si, 2 * k * P : 2 * (k + 1) * P].bitcast(E2M1),
+                        lhsT_scale=w1s_t[:, e * SI + si, k * P : (k + 1) * P],
+                        rhs=da_codes[si][:].bitcast(E5M2),
+                        rhs_scale=da_scales[si][:],
+                        start=(si == 0),
+                        stop=(si == SI - 1),
+                    )
+                d = held.tile([P, C], F32, name=f"dx{e}{k}")
+                nc.scalar.activation(out=d[:], in_=acc[:], func=COPY, scale=2.0)
+                dx[e, k] = d
+
+        def scatter(e, k, lo, hi):
+            o = offsets[:, (e * C + lo) // 16 : (e * C + hi) // 16]
+            nc.vector.tensor_copy(win[k][:].indirect(o), dx[e, k][:, lo:hi])
+
+        permute_w2_words(0)
+        gather_and_quantize(0, 0)
+        permute_w2_scales(0)
+        gather_and_quantize(0, 1)
+        layers(0)
+        gather_and_quantize(1, 0)
+        permute_w2_words(1)
+        permute_w2_scales(1)
+        gather_and_quantize(1, 1)
+        layers(1)
+        for k in range(KT):
+            for lo in range(0, C, C // 2):
+                scatter(0, k, lo, lo + C // 2)
+        for k in range(KT):
+            scatter(1, k, 0, C)
+            nc.sync.dma_start(out[k * P : (k + 1) * P, :], win[k][:])

@@ -18,6 +18,7 @@ U8 = mybir.dt.uint8
 E5M2 = mybir.dt.float8_e5m2_x4
 E2M1 = mybir.dt.float4_e2m1fn_x4
 ALU = mybir.AluOpType
+RELU = mybir.ActivationFunctionType.Relu
 COPY = mybir.ActivationFunctionType.Copy
 
 
@@ -26,11 +27,10 @@ def tile_moe_bdx_mlp_relu2_kernel(
 ):
     nc = tc.nc
     SN, SI, KT = N // PASS, H // PASS, K // P
-    last = E - 1
+
+    POOL = {}
 
     def cuts(e, s):
-        if e == last and s == 1:
-            return [(0, C // 2), (C // 2, C)]
         return [(0, C)]
 
     with ExitStack() as ctx:
@@ -43,8 +43,8 @@ def tile_moe_bdx_mlp_relu2_kernel(
         a_t = [[held.tile([P, PACK, C], F32, name=f"a{e}{s}") for s in range(SI)] for e in range(E)]
         w2_raw = [held.tile([P, SN, 2 * H], U8, name=f"w2r{e}", align_bytes=64) for e in range(E)]
         w2_p = [held.tile([P, SN, 2 * H], U8, name=f"w2p{e}", align_bytes=64) for e in range(E)]
-        w2s_raw = held.tile([P, E * SN, H], U8, name="w2sr", align_bytes=64)
-        w2s_p = [held.tile([P, SN, H], U8, name=f"w2sp{e}", align_bytes=64) for e in range(E)]
+        w2s_raw = held.tile([P, H], U8, name="w2sr", align_bytes=64)
+        w2s_p = [held.tile([P, H], U8, name=f"w2sp{j}", align_bytes=64) for j in range(E * SN)]
         w1_t = held.tile([P, E * SI, 2 * K], U8, name="w1t", align_bytes=64)
         w1s_t = held.tile([P, E * SI, K], U8, name="w1s", align_bytes=64)
         win = [held.tile([P, T], F32, name=f"win{k}") for k in range(KT)]
@@ -52,13 +52,15 @@ def tile_moe_bdx_mlp_relu2_kernel(
         dy_v = dyT.rearrange("(s p t) c -> s t p c", p=P, t=PACK)
         a_v = a.rearrange("(s p t) (e c) -> e s p t c", p=P, t=PACK, e=E)
         w2_v = w2_words.bitcast(I32)
-        w2s_v = w2_scales.bitcast(I32).rearrange("e s f i -> f (e s) i")
+        w2s_v = w2_scales.bitcast(I32).rearrange("e s f i -> (e s) f i")
         w1_v = w1_words.bitcast(I32).rearrange("e s p b -> p (e s) b")
         w1s_v = w1_scales.bitcast(I32).rearrange("e s f i -> f (e s) i")
 
         nc.sync.dma_start(offsets[:], offs)
         nc.vector.memset(w2s_raw[:].bitcast(I32), 0)
         nc.vector.memset(w1s_t[:].bitcast(I32), 0)
+        for j in range(1, E * SN):
+            nc.gpsimd.memset(w2s_p[j][:].bitcast(I32), 0)
 
         def load_w2(e):
             for s in range(SN):
@@ -69,15 +71,15 @@ def tile_moe_bdx_mlp_relu2_kernel(
         for t in range(PACK):
             nc.sync.dma_start(dy_t[0][t][:], dy_v[0, t])
         for q in range(4):
-            nc.sync.dma_start(w2s_raw[32 * q : 32 * q + 4, :, :].bitcast(I32), w2s_v[4 * q : 4 * q + 4])
+            nc.sync.dma_start(w2s_raw[32 * q : 32 * q + 16, :].bitcast(I32), w2s_v[:, 4 * q : 4 * q + 4])
         for t in range(PACK):
             nc.sync.dma_start(dy_t[1][t][:], dy_v[1, t])
+        nc.sync.dma_start(gate_t[1][:], gate[0:P, C : 2 * C])
         nc.sync.dma_start(w1_t[:].bitcast(I32), w1_v)
         for q in range(4):
             nc.sync.dma_start(w1s_t[32 * q : 32 * q + 4, :, :].bitcast(I32), w1s_v[4 * q : 4 * q + 4])
         for s in range(SI):
             nc.sync.dma_start(a_t[0][s][:], a_v[0, s])
-        nc.sync.dma_start(gate_t[1][:], gate[0:P, C : 2 * C])
         load_w2(1)
         for s in range(SI):
             nc.sync.dma_start(a_t[1][s][:], a_v[1, s])
@@ -89,11 +91,14 @@ def tile_moe_bdx_mlp_relu2_kernel(
                     in_=w2_raw[e][:, s, :].bitcast(U16).rearrange("p (s m t) -> p s t m", s=SI, t=PACK),
                 )
 
-        def permute_w2_scales(e):
+        def permute_w2_scales():
             nc.vector.tensor_copy(
-                out=w2s_p[e][:].rearrange("p n (s t m) -> p (n s) t m", s=SI, t=PACK),
-                in_=w2s_raw[:, e * SN : (e + 1) * SN, :].rearrange("p n (s m t) -> p (n s) t m", s=SI, t=PACK),
+                out=w2s_p[0][:].rearrange("p (s t m) -> p s t m", s=SI, t=PACK),
+                in_=w2s_raw[:].rearrange("p (s m t) -> p s t m", s=SI, t=PACK),
             )
+            for j in range(1, E * SN):
+                for r in range(4):
+                    nc.sync.dma_start(w2s_p[j][r:P:32, :].bitcast(I32), w2s_p[0][4 * j + r : P : 32, :].bitcast(I32))
 
         g_codes = {}
         g_scales = {}
@@ -116,55 +121,86 @@ def tile_moe_bdx_mlp_relu2_kernel(
 
         dx = {}
 
-        def layers(e):
-            da_codes = []
-            da_scales = []
+        relu_a = {}
+
+        def relu_for_pool(e):
             for si in range(SI):
-                da = held.tile([P, PACK, C], BF16, name=f"da{e}{si}")
-                dai = held.tile([P, C, PACK], BF16, name=f"dai{e}{si}", align_bytes=64)
-                codes = held.tile([P, C], U32, name=f"dc{e}{si}", align_bytes=64)
-                scales = held.tile([P, C], U8, name=f"ds{e}{si}", align_bytes=64)
-                banks = []
+                for t in POOL.get((e, si), ()):
+                    r = held.tile([P, C], F32, name=f"ra{e}{si}{t}")
+                    nc.scalar.activation(out=r[:], in_=a_t[e][si][:, t, :], func=RELU)
+                    relu_a[e, si, t] = r
+
+        banks = {}
+        acc = {}
+        ring = [0]
+
+        def first(e, j, s):
+            if s == 0:
+                banks[e, j] = psum.tile([P, C], F32, name=f"dh{ring[0] % 6}")
+                ring[0] += 1
+            nc.tensor.matmul_mx(
+                out=banks[e, j][:],
+                lhsT=w2_p[e][:, s, 2 * j * P : 2 * (j + 1) * P].bitcast(E2M1),
+                lhsT_scale=w2s_p[e * SN + s][:, j * P : (j + 1) * P],
+                rhs=g_codes[e, s][:].bitcast(E5M2),
+                rhs_scale=g_scales[e, s][:],
+                start=(s == 0),
+                stop=(s == SN - 1),
+            )
+
+        def first_passes(e):
+            for j in range(6):
+                first(e, j, 0)
+
+        def layer(e, si):
+            pool_planes = POOL.get((e, si), ())
+            if si == 0:
+                for k in range(KT):
+                    acc[k] = psum.tile([P, C], F32, name=f"acc{k}")
+            da = held.tile([P, PACK, C], BF16, name=f"da{e}{si}")
+            dai = held.tile([P, C, PACK], BF16, name=f"dai{e}{si}", align_bytes=64)
+            codes = held.tile([P, C], U32, name=f"dc{e}{si}", align_bytes=64)
+            scales = held.tile([P, C], U8, name=f"ds{e}{si}", align_bytes=64)
+            order = [t for t in pool_planes] + [t for t in range(PACK) if t not in pool_planes]
+            for t in order:
+                j = si * PACK + t
+                if (e, j) not in banks:
+                    first(e, j, 0)
+                first(e, j, 1)
+            for t in pool_planes:
+                d = held.tile([P, C], F32, name=f"dhs{e}{si}{t}")
+                nc.scalar.copy(out=d[:], in_=banks[e, si * PACK + t][:])
+                nc.gpsimd.tensor_tensor(da[:, t, :], d[:], relu_a[e, si, t][:], ALU.mult)
+            for lo, hi in cuts(e, si):
                 for t in range(PACK):
-                    m0 = (si * PACK + t) * P
-                    dh = psum.tile([P, C], F32, name=f"dh{(si * PACK + t) % 6}")
-                    for s in range(SN):
-                        nc.tensor.matmul_mx(
-                            out=dh[:],
-                            lhsT=w2_p[e][:, s, 2 * m0 : 2 * (m0 + P)].bitcast(E2M1),
-                            lhsT_scale=w2s_p[e][:, s, m0 : m0 + P],
-                            rhs=g_codes[e, s][:].bitcast(E5M2),
-                            rhs_scale=g_scales[e, s][:],
-                            start=(s == 0),
-                            stop=(s == SN - 1),
-                        )
-                    banks.append(dh)
-                for lo, hi in cuts(e, si):
-                    for t in range(PACK):
+                    if t not in pool_planes:
                         nc.vector.scalar_tensor_tensor(
-                            out=da[:, t, lo:hi], in0=a_t[e][si][:, t, lo:hi], scalar=0.0, in1=banks[t][:, lo:hi], op0=ALU.max, op1=ALU.mult
+                            out=da[:, t, lo:hi],
+                            in0=a_t[e][si][:, t, lo:hi],
+                            scalar=0.0,
+                            in1=banks[e, si * PACK + t][:, lo:hi],
+                            op0=ALU.max,
+                            op1=ALU.mult,
                         )
-                    nc.scalar.copy(out=dai[:, lo:hi, :], in_=da[:, :, lo:hi].rearrange("p t c -> p c t"))
-                    nc.vector.quantize_mx(
-                        out=codes[:, lo:hi].bitcast(E5M2), scales=scales[:, lo:hi], in_=dai[:, lo:hi, :].rearrange("p c t -> p (c t)")
-                    )
-                da_codes.append(codes)
-                da_scales.append(scales)
+                nc.scalar.copy(out=dai[:, lo:hi, :], in_=da[:, :, lo:hi].rearrange("p t c -> p c t"))
+                nc.vector.quantize_mx(
+                    out=codes[:, lo:hi].bitcast(E5M2), scales=scales[:, lo:hi], in_=dai[:, lo:hi, :].rearrange("p c t -> p (c t)")
+                )
             for k in range(KT):
-                acc = psum.tile([P, C], F32, name=f"acc{k}")
-                for si in range(SI):
-                    nc.tensor.matmul_mx(
-                        out=acc[:],
-                        lhsT=w1_t[:, e * SI + si, 2 * k * P : 2 * (k + 1) * P].bitcast(E2M1),
-                        lhsT_scale=w1s_t[:, e * SI + si, k * P : (k + 1) * P],
-                        rhs=da_codes[si][:].bitcast(E5M2),
-                        rhs_scale=da_scales[si][:],
-                        start=(si == 0),
-                        stop=(si == SI - 1),
-                    )
-                d = held.tile([P, C], F32, name=f"dx{e}{k}")
-                nc.scalar.activation(out=d[:], in_=acc[:], func=COPY, scale=2.0)
-                dx[e, k] = d
+                nc.tensor.matmul_mx(
+                    out=acc[k][:],
+                    lhsT=w1_t[:, e * SI + si, 2 * k * P : 2 * (k + 1) * P].bitcast(E2M1),
+                    lhsT_scale=w1s_t[:, e * SI + si, k * P : (k + 1) * P],
+                    rhs=codes[:].bitcast(E5M2),
+                    rhs_scale=scales[:],
+                    start=(si == 0),
+                    stop=(si == SI - 1),
+                )
+            if si == SI - 1:
+                for k in range(KT):
+                    d = held.tile([P, C], F32, name=f"dx{e}{k}")
+                    nc.scalar.activation(out=d[:], in_=acc[k][:], func=COPY, scale=2.0)
+                    dx[e, k] = d
 
         def scatter(e, k, lo, hi):
             o = offsets[:, (e * C + lo) // 16 : (e * C + hi) // 16]
@@ -172,14 +208,19 @@ def tile_moe_bdx_mlp_relu2_kernel(
 
         permute_w2_words(0)
         gather_and_quantize(0, 0)
-        permute_w2_scales(0)
+        permute_w2_scales()
         gather_and_quantize(0, 1)
-        layers(0)
+        relu_for_pool(0)
+        relu_for_pool(1)
+        first_passes(0)
+        layer(0, 0)
         gather_and_quantize(1, 0)
-        permute_w2_words(1)
-        permute_w2_scales(1)
         gather_and_quantize(1, 1)
-        layers(1)
+        permute_w2_words(1)
+        layer(0, 1)
+        first_passes(1)
+        layer(1, 0)
+        layer(1, 1)
         for k in range(KT):
             for lo in range(0, C, C // 2):
                 scatter(0, k, lo, lo + C // 2)

@@ -18,7 +18,6 @@ U8 = mybir.dt.uint8
 E5M2 = mybir.dt.float8_e5m2_x4
 E2M1 = mybir.dt.float4_e2m1fn_x4
 ALU = mybir.AluOpType
-RELU = mybir.ActivationFunctionType.Relu
 COPY = mybir.ActivationFunctionType.Copy
 
 
@@ -28,10 +27,6 @@ def tile_moe_bdx_mlp_relu2_kernel(
     nc = tc.nc
     SN, SI, KT = N // PASS, H // PASS, K // P
 
-    POOL = {}
-
-    def cuts(e, s):
-        return [(0, C)]
 
     with ExitStack() as ctx:
         held = ctx.enter_context(tc.tile_pool(name="held", bufs=1))
@@ -51,7 +46,7 @@ def tile_moe_bdx_mlp_relu2_kernel(
 
         dy_v = dyT.rearrange("(s p t) c -> s t p c", p=P, t=PACK)
         a_v = a.rearrange("(s p t) (e c) -> e s p t c", p=P, t=PACK, e=E)
-        w2_v = w2_words.bitcast(I32)
+        w2_v = w2_words.bitcast(I32).rearrange("e s p b -> e p s b")
         w2s_v = w2_scales.bitcast(I32).rearrange("e s f i -> (e s) f i")
         w1_v = w1_words.bitcast(I32).rearrange("e s p b -> p (e s) b")
         w1s_v = w1_scales.bitcast(I32).rearrange("e s f i -> f (e s) i")
@@ -63,15 +58,14 @@ def tile_moe_bdx_mlp_relu2_kernel(
             nc.gpsimd.memset(w2s_p[j][:].bitcast(I32), 0)
 
         def load_w2(e):
-            for s in range(SN):
-                nc.sync.dma_start(w2_raw[e][:, s, :].bitcast(I32), w2_v[e, s])
+            nc.sync.dma_start(w2_raw[e][:].bitcast(I32), w2_v[e])
 
         load_w2(0)
+        for q in range(4):
+            nc.sync.dma_start(w2s_raw[32 * q : 32 * q + 16, :].bitcast(I32), w2s_v[:, 4 * q : 4 * q + 4])
         nc.sync.dma_start(gate_t[0][:], gate[0:P, 0:C])
         for t in range(PACK):
             nc.sync.dma_start(dy_t[0][t][:], dy_v[0, t])
-        for q in range(4):
-            nc.sync.dma_start(w2s_raw[32 * q : 32 * q + 16, :].bitcast(I32), w2s_v[:, 4 * q : 4 * q + 4])
         for t in range(PACK):
             nc.sync.dma_start(dy_t[1][t][:], dy_v[1, t])
         nc.sync.dma_start(gate_t[1][:], gate[0:P, C : 2 * C])
@@ -85,11 +79,10 @@ def tile_moe_bdx_mlp_relu2_kernel(
             nc.sync.dma_start(a_t[1][s][:], a_v[1, s])
 
         def permute_w2_words(e):
-            for s in range(SN):
-                nc.vector.tensor_copy(
-                    out=w2_p[e][:, s, :].bitcast(U16).rearrange("p (s t m) -> p s t m", s=SI, t=PACK),
-                    in_=w2_raw[e][:, s, :].bitcast(U16).rearrange("p (s m t) -> p s t m", s=SI, t=PACK),
-                )
+            nc.vector.tensor_copy(
+                out=w2_p[e][:].bitcast(U16).rearrange("p n (s t m) -> p (n s) t m", s=SI, t=PACK),
+                in_=w2_raw[e][:].bitcast(U16).rearrange("p n (s m t) -> p (n s) t m", s=SI, t=PACK),
+            )
 
         def permute_w2_scales():
             nc.vector.tensor_copy(
@@ -100,44 +93,39 @@ def tile_moe_bdx_mlp_relu2_kernel(
                 for r in range(4):
                     nc.sync.dma_start(w2s_p[j][r:P:32, :].bitcast(I32), w2s_p[0][4 * j + r : P : 32, :].bitcast(I32))
 
-        g_codes = {}
-        g_scales = {}
+        def interleave(dst, src):
+            nc.scalar.copy(
+                out=dst[:].rearrange("p (c i) t -> p c t i", i=4),
+                in_=src[:].rearrange("p t (c i) -> p c t i", i=4),
+            )
 
-        def gather_and_quantize(e, s):
-            g = held.tile([P, PACK, C], F32, name=f"g{e}{s}")
-            gi = held.tile([P, C, PACK], BF16, name=f"gi{e}{s}", align_bytes=64)
-            codes = held.tile([P, C], U32, name=f"gc{e}{s}", align_bytes=64)
-            scales = held.tile([P, C], U8, name=f"gs{e}{s}", align_bytes=64)
-            for lo, hi in cuts(e, s):
-                o = offsets[:, (e * C + lo) // 16 : (e * C + hi) // 16]
-                for t in range(PACK):
-                    nc.vector.tensor_tensor(g[:, t, lo:hi], dy_t[s][t][:].indirect(o), gate_t[e][:, lo:hi], ALU.mult)
-                nc.scalar.copy(out=gi[:, lo:hi, :], in_=g[:, :, lo:hi].rearrange("p t c -> p c t"))
-                nc.vector.quantize_mx(
-                    out=codes[:, lo:hi].bitcast(E5M2), scales=scales[:, lo:hi], in_=gi[:, lo:hi, :].rearrange("p c t -> p (c t)")
-                )
-            g_codes[e, s] = codes
-            g_scales[e, s] = scales
+        def quantize(codes, scales, src):
+            nc.vector.quantize_mx(out=codes[:].bitcast(E5M2), scales=scales[:], in_=src[:].rearrange("p c t -> p (c t)"))
 
-        dx = {}
-
-        relu_a = {}
-
-        def relu_for_pool(e):
-            for si in range(SI):
-                for t in POOL.get((e, si), ()):
-                    r = held.tile([P, C], F32, name=f"ra{e}{si}{t}")
-                    nc.scalar.activation(out=r[:], in_=a_t[e][si][:, t, :], func=RELU)
-                    relu_a[e, si, t] = r
-
+        pairs = [(e, s) for e in range(E) for s in range(2)]
+        g = {x: held.tile([P, PACK, C], F32, name=f"g{x[0]}{x[1]}") for x in pairs}
+        gi = {x: held.tile([P, C, PACK], BF16, name=f"gi{x[0]}{x[1]}", align_bytes=64) for x in pairs}
+        g_codes = {x: held.tile([P, C], U32, name=f"gc{x[0]}{x[1]}", align_bytes=64) for x in pairs}
+        g_scales = {x: held.tile([P, C], U8, name=f"gs{x[0]}{x[1]}", align_bytes=64) for x in pairs}
+        da = {x: held.tile([P, PACK, C], BF16, name=f"da{x[0]}{x[1]}") for x in pairs}
+        dai = {x: held.tile([P, C, PACK], BF16, name=f"dai{x[0]}{x[1]}", align_bytes=64) for x in pairs}
+        da_codes = {x: held.tile([P, C], U32, name=f"dc{x[0]}{x[1]}", align_bytes=64) for x in pairs}
+        da_scales = {x: held.tile([P, C], U8, name=f"ds{x[0]}{x[1]}", align_bytes=64) for x in pairs}
+        dx = {(e, k): held.tile([P, C], F32, name=f"dx{e}{k}") for e in range(E) for k in range(KT)}
         banks = {}
-        acc = {}
-        ring = [0]
+
+        def gather(e, s, t):
+            o = offsets[:, e * C // 16 : (e + 1) * C // 16]
+            nc.vector.tensor_tensor(g[e, s][:, t, :], dy_t[s][t][:].indirect(o), gate_t[e][:], ALU.mult)
+            if t == PACK - 1:
+                interleave(gi[e, s], g[e, s])
+
+        def quantize_g(e, s):
+            quantize(g_codes[e, s], g_scales[e, s], gi[e, s])
 
         def first(e, j, s):
             if s == 0:
-                banks[e, j] = psum.tile([P, C], F32, name=f"dh{ring[0] % 6}")
-                ring[0] += 1
+                banks[e, j] = psum.tile([P, C], F32, name=f"dh{(e * SI * PACK + j) % 6}")
             nc.tensor.matmul_mx(
                 out=banks[e, j][:],
                 lhsT=w2_p[e][:, s, 2 * j * P : 2 * (j + 1) * P].bitcast(E2M1),
@@ -148,82 +136,73 @@ def tile_moe_bdx_mlp_relu2_kernel(
                 stop=(s == SN - 1),
             )
 
-        def first_passes(e):
-            for j in range(6):
+        def derive(e, j):
+            si, t = divmod(j, PACK)
+            if (e, j) not in banks:
                 first(e, j, 0)
+            first(e, j, 1)
+            nc.vector.scalar_tensor_tensor(
+                out=da[e, si][:, t, :], in0=a_t[e][si][:, t, :], scalar=0.0, in1=banks[e, j][:], op0=ALU.max, op1=ALU.mult
+            )
+            if t == PACK - 1:
+                interleave(dai[e, si], da[e, si])
 
-        def layer(e, si):
-            pool_planes = POOL.get((e, si), ())
-            if si == 0:
-                for k in range(KT):
-                    acc[k] = psum.tile([P, C], F32, name=f"acc{k}")
-            da = held.tile([P, PACK, C], BF16, name=f"da{e}{si}")
-            dai = held.tile([P, C, PACK], BF16, name=f"dai{e}{si}", align_bytes=64)
-            codes = held.tile([P, C], U32, name=f"dc{e}{si}", align_bytes=64)
-            scales = held.tile([P, C], U8, name=f"ds{e}{si}", align_bytes=64)
-            order = [t for t in pool_planes] + [t for t in range(PACK) if t not in pool_planes]
-            for t in order:
-                j = si * PACK + t
-                if (e, j) not in banks:
-                    first(e, j, 0)
-                first(e, j, 1)
-            for t in pool_planes:
-                d = held.tile([P, C], F32, name=f"dhs{e}{si}{t}")
-                nc.scalar.copy(out=d[:], in_=banks[e, si * PACK + t][:])
-                nc.gpsimd.tensor_tensor(da[:, t, :], d[:], relu_a[e, si, t][:], ALU.mult)
-            for lo, hi in cuts(e, si):
-                for t in range(PACK):
-                    if t not in pool_planes:
-                        nc.vector.scalar_tensor_tensor(
-                            out=da[:, t, lo:hi],
-                            in0=a_t[e][si][:, t, lo:hi],
-                            scalar=0.0,
-                            in1=banks[e, si * PACK + t][:, lo:hi],
-                            op0=ALU.max,
-                            op1=ALU.mult,
-                        )
-                nc.scalar.copy(out=dai[:, lo:hi, :], in_=da[:, :, lo:hi].rearrange("p t c -> p c t"))
-                nc.vector.quantize_mx(
-                    out=codes[:, lo:hi].bitcast(E5M2), scales=scales[:, lo:hi], in_=dai[:, lo:hi, :].rearrange("p c t -> p (c t)")
-                )
+        def second(e, si):
+            quantize(da_codes[e, si], da_scales[e, si], dai[e, si])
             for k in range(KT):
+                if si == 0:
+                    banks[e, "x", k] = psum.tile([P, C], F32, name=f"acc{k}")
                 nc.tensor.matmul_mx(
-                    out=acc[k][:],
+                    out=banks[e, "x", k][:],
                     lhsT=w1_t[:, e * SI + si, 2 * k * P : 2 * (k + 1) * P].bitcast(E2M1),
                     lhsT_scale=w1s_t[:, e * SI + si, k * P : (k + 1) * P],
-                    rhs=codes[:].bitcast(E5M2),
-                    rhs_scale=scales[:],
+                    rhs=da_codes[e, si][:].bitcast(E5M2),
+                    rhs_scale=da_scales[e, si][:],
                     start=(si == 0),
                     stop=(si == SI - 1),
                 )
-            if si == SI - 1:
-                for k in range(KT):
-                    d = held.tile([P, C], F32, name=f"dx{e}{k}")
-                    nc.scalar.activation(out=d[:], in_=acc[k][:], func=COPY, scale=2.0)
-                    dx[e, k] = d
+                if si == SI - 1:
+                    nc.scalar.activation(out=dx[e, k][:], in_=banks[e, "x", k][:], func=COPY, scale=2.0)
 
-        def scatter(e, k, lo, hi):
-            o = offsets[:, (e * C + lo) // 16 : (e * C + hi) // 16]
-            nc.vector.tensor_copy(win[k][:].indirect(o), dx[e, k][:, lo:hi])
+        def scatter(e, k):
+            nc.vector.tensor_copy(win[k][:].indirect(offsets[:, e * C // 16 : (e + 1) * C // 16]), dx[e, k][:])
 
         permute_w2_words(0)
-        gather_and_quantize(0, 0)
         permute_w2_scales()
-        gather_and_quantize(0, 1)
-        relu_for_pool(0)
-        relu_for_pool(1)
-        first_passes(0)
-        layer(0, 0)
-        gather_and_quantize(1, 0)
-        gather_and_quantize(1, 1)
+        for s in range(SN):
+            for t in range(PACK):
+                gather(0, s, t)
+        quantize_g(0, 0)
+        for j in range(6):
+            first(0, j, 0)
+        for t in range(3):
+            gather(1, 0, t)
+        quantize_g(0, 1)
+        gather(1, 0, 3)
+        for j in range(4):
+            derive(0, j)
+        for t in range(3):
+            gather(1, 1, t)
+        quantize_g(1, 0)
+        gather(1, 1, 3)
+        second(0, 0)
         permute_w2_words(1)
-        layer(0, 1)
-        first_passes(1)
-        layer(1, 0)
-        layer(1, 1)
+        for j in range(4, 6):
+            derive(0, j)
+        quantize_g(1, 1)
+        for j in range(6, 8):
+            derive(0, j)
+        for j in range(6):
+            first(1, j, 0)
+        for j in range(5):
+            derive(1, j)
+        second(0, 1)
+        for j in range(5, 8):
+            derive(1, j)
+        second(1, 0)
+        scatter(0, 0)
+        second(1, 1)
+        scatter(0, 1)
         for k in range(KT):
-            for lo in range(0, C, C // 2):
-                scatter(0, k, lo, lo + C // 2)
-        for k in range(KT):
-            scatter(1, k, 0, C)
+            scatter(1, k)
             nc.sync.dma_start(out[k * P : (k + 1) * P, :], win[k][:])

@@ -61,13 +61,13 @@ def tile_moe_bdx_mlp_relu2_kernel(
             nc.sync.dma_start(w2_raw[e][:].bitcast(I32), w2_v[e])
 
         load_w2(0)
-        for q in range(4):
-            nc.sync.dma_start(w2s_raw[32 * q : 32 * q + 16, :].bitcast(I32), w2s_v[:, 4 * q : 4 * q + 4])
         nc.sync.dma_start(gate_t[0][:], gate[0:P, 0:C])
         for t in range(PACK):
             nc.sync.dma_start(dy_t[0][t][:], dy_v[0, t])
         for t in range(PACK):
             nc.sync.dma_start(dy_t[1][t][:], dy_v[1, t])
+        for q in range(4):
+            nc.sync.dma_start(w2s_raw[32 * q : 32 * q + 16, :].bitcast(I32), w2s_v[:, 4 * q : 4 * q + 4])
         nc.sync.dma_start(gate_t[1][:], gate[0:P, C : 2 * C])
         nc.sync.dma_start(w1_t[:].bitcast(I32), w1_v)
         for q in range(4):
@@ -168,10 +168,10 @@ def tile_moe_bdx_mlp_relu2_kernel(
             nc.vector.tensor_copy(win[k][:].indirect(offsets[:, e * C // 16 : (e + 1) * C // 16]), dx[e, k][:])
 
         permute_w2_words(0)
-        permute_w2_scales()
         for s in range(SN):
             for t in range(PACK):
                 gather(0, s, t)
+        permute_w2_scales()
         quantize_g(0, 0)
         for j in range(6):
             first(0, j, 0)

from contextlib import ExitStack

import concourse.mybir as mybir

K, T, E, C, H, N = 256, 1024, 2, 512, 1024, 1024
P = 128
PACK = 4
PASS = P * PACK
FLOPS = 2 * E * C * H * (N + K)
BYTES = 4 * (N * T + H * E * C + K * T + E * C) + E * N * H // 2 + E * H * K // 2 + E * N * H // 32 + E * H * K // 32 + 2 * E * C

F32 = mybir.dt.float32
BF16 = mybir.dt.bfloat16
I32 = mybir.dt.int32
U32 = mybir.dt.uint32
U16 = mybir.dt.uint16
U8 = mybir.dt.uint8
E5M2 = mybir.dt.float8_e5m2_x4
E2M1 = mybir.dt.float4_e2m1fn_x4
ALU = mybir.AluOpType
COPY = mybir.ActivationFunctionType.Copy


def tile_moe_bdx_mlp_relu2_kernel(
    tc, dyT, a, w2_words, w2_scales, w1_words, w1_scales, gate, offs, out
):
    nc = tc.nc
    SN, SI, KT = N // PASS, H // PASS, K // P


    with ExitStack() as ctx:
        held = ctx.enter_context(tc.tile_pool(name="held", bufs=1))
        psum = ctx.enter_context(tc.psum_pool(name="psum", bufs=1))

        offsets = held.tile([P, E * C // 16], U16, name="offsets")
        dy_t = [[held.tile([P, T], F32, name=f"dy{s}{t}") for t in range(PACK)] for s in range(SN)]
        gate_t = [held.tile([P, C], F32, name=f"gate{e}") for e in range(E)]
        a_t = [[held.tile([P, PACK, C], F32, name=f"a{e}{s}") for s in range(SI)] for e in range(E)]
        w2_raw = [held.tile([P, SN, 2 * H], U8, name=f"w2r{e}", align_bytes=64) for e in range(E)]
        w2_p = [held.tile([P, SN, 2 * H], U8, name=f"w2p{e}", align_bytes=64) for e in range(E)]
        w2s_raw = held.tile([P, H], U8, name="w2sr", align_bytes=64)
        w2s_p = [held.tile([P, H], U8, name=f"w2sp{j}", align_bytes=64) for j in range(E * SN)]
        w1_t = held.tile([P, E * SI, 2 * K], U8, name="w1t", align_bytes=64)
        w1s_t = held.tile([P, E * SI, K], U8, name="w1s", align_bytes=64)
        win = [held.tile([P, T], F32, name=f"win{k}") for k in range(KT)]

        dy_v = dyT.rearrange("(s p t) c -> s t p c", p=P, t=PACK)
        a_v = a.rearrange("(s p t) (e c) -> e s p t c", p=P, t=PACK, e=E)
        w2_v = w2_words.bitcast(I32).rearrange("e s p b -> e p s b")
        w2s_v = w2_scales.bitcast(I32).rearrange("e s f i -> (e s) f i")
        w1_v = w1_words.bitcast(I32).rearrange("e s p b -> p (e s) b")
        w1s_v = w1_scales.bitcast(I32).rearrange("e s f i -> f (e s) i")

        nc.sync.dma_start(offsets[:], offs)
        nc.vector.memset(w2s_raw[:].bitcast(I32), 0)
        nc.vector.memset(w1s_t[:].bitcast(I32), 0)
        for j in range(1, E * SN):
            nc.gpsimd.memset(w2s_p[j][:].bitcast(I32), 0)

        def load_w2(e):
            nc.sync.dma_start(w2_raw[e][:].bitcast(I32), w2_v[e])

        load_w2(0)
        nc.sync.dma_start(gate_t[0][:], gate[0:P, 0:C])
        for t in range(PACK):
            nc.sync.dma_start(dy_t[0][t][:], dy_v[0, t])
        for t in range(PACK):
            nc.sync.dma_start(dy_t[1][t][:], dy_v[1, t])
        for q in range(4):
            nc.sync.dma_start(w2s_raw[32 * q : 32 * q + 16, :].bitcast(I32), w2s_v[:, 4 * q : 4 * q + 4])
        nc.sync.dma_start(gate_t[1][:], gate[0:P, C : 2 * C])
        nc.sync.dma_start(w1_t[:].bitcast(I32), w1_v)
        for q in range(4):
            nc.sync.dma_start(w1s_t[32 * q : 32 * q + 4, :, :].bitcast(I32), w1s_v[4 * q : 4 * q + 4])
        for s in range(SI):
            nc.sync.dma_start(a_t[0][s][:], a_v[0, s])
        load_w2(1)
        for s in range(SI):
            nc.sync.dma_start(a_t[1][s][:], a_v[1, s])

        def permute_w2_words(e):
            nc.vector.tensor_copy(
                out=w2_p[e][:].bitcast(U16).rearrange("p n (s t m) -> p (n s) t m", s=SI, t=PACK),
                in_=w2_raw[e][:].bitcast(U16).rearrange("p n (s m t) -> p (n s) t m", s=SI, t=PACK),
            )

        def permute_w2_scales():
            nc.vector.tensor_copy(
                out=w2s_p[0][:].rearrange("p (s t m) -> p s t m", s=SI, t=PACK),
                in_=w2s_raw[:].rearrange("p (s m t) -> p s t m", s=SI, t=PACK),
            )
            for j in range(1, E * SN):
                for r in range(4):
                    nc.sync.dma_start(w2s_p[j][r:P:32, :].bitcast(I32), w2s_p[0][4 * j + r : P : 32, :].bitcast(I32))

        def interleave(dst, src):
            nc.scalar.copy(
                out=dst[:].rearrange("p (c i) t -> p c t i", i=4),
                in_=src[:].rearrange("p t (c i) -> p c t i", i=4),
            )

        def quantize(codes, scales, src):
            nc.vector.quantize_mx(out=codes[:].bitcast(E5M2), scales=scales[:], in_=src[:].rearrange("p c t -> p (c t)"))

        pairs = [(e, s) for e in range(E) for s in range(2)]
        g = {x: held.tile([P, PACK, C], F32, name=f"g{x[0]}{x[1]}") for x in pairs}
        gi = {x: held.tile([P, C, PACK], BF16, name=f"gi{x[0]}{x[1]}", align_bytes=64) for x in pairs}
        g_codes = {x: held.tile([P, C], U32, name=f"gc{x[0]}{x[1]}", align_bytes=64) for x in pairs}
        g_scales = {x: held.tile([P, C], U8, name=f"gs{x[0]}{x[1]}", align_bytes=64) for x in pairs}
        da = {x: held.tile([P, PACK, C], BF16, name=f"da{x[0]}{x[1]}") for x in pairs}
        dai = {x: held.tile([P, C, PACK], BF16, name=f"dai{x[0]}{x[1]}", align_bytes=64) for x in pairs}
        da_codes = {x: held.tile([P, C], U32, name=f"dc{x[0]}{x[1]}", align_bytes=64) for x in pairs}
        da_scales = {x: held.tile([P, C], U8, name=f"ds{x[0]}{x[1]}", align_bytes=64) for x in pairs}
        dx = {(e, k): held.tile([P, C], F32, name=f"dx{e}{k}") for e in range(E) for k in range(KT)}
        banks = {}

        def gather(e, s, t):
            o = offsets[:, e * C // 16 : (e + 1) * C // 16]
            nc.vector.tensor_tensor(g[e, s][:, t, :], dy_t[s][t][:].indirect(o), gate_t[e][:], ALU.mult)
            if t == PACK - 1:
                interleave(gi[e, s], g[e, s])

        def quantize_g(e, s):
            quantize(g_codes[e, s], g_scales[e, s], gi[e, s])

        def first(e, j, s):
            if s == 0:
                banks[e, j] = psum.tile([P, C], F32, name=f"dh{(e * SI * PACK + j) % 6}")
            nc.tensor.matmul_mx(
                out=banks[e, j][:],
                lhsT=w2_p[e][:, s, 2 * j * P : 2 * (j + 1) * P].bitcast(E2M1),
                lhsT_scale=w2s_p[e * SN + s][:, j * P : (j + 1) * P],
                rhs=g_codes[e, s][:].bitcast(E5M2),
                rhs_scale=g_scales[e, s][:],
                start=(s == 0),
                stop=(s == SN - 1),
            )

        def derive(e, j):
            si, t = divmod(j, PACK)
            if (e, j) not in banks:
                first(e, j, 0)
            first(e, j, 1)
            nc.vector.scalar_tensor_tensor(
                out=da[e, si][:, t, :], in0=a_t[e][si][:, t, :], scalar=0.0, in1=banks[e, j][:], op0=ALU.max, op1=ALU.mult
            )
            if t == PACK - 1:
                interleave(dai[e, si], da[e, si])

        def second(e, si):
            quantize(da_codes[e, si], da_scales[e, si], dai[e, si])
            for k in range(KT):
                if si == 0:
                    banks[e, "x", k] = psum.tile([P, C], F32, name=f"acc{k}")
                nc.tensor.matmul_mx(
                    out=banks[e, "x", k][:],
                    lhsT=w1_t[:, e * SI + si, 2 * k * P : 2 * (k + 1) * P].bitcast(E2M1),
                    lhsT_scale=w1s_t[:, e * SI + si, k * P : (k + 1) * P],
                    rhs=da_codes[e, si][:].bitcast(E5M2),
                    rhs_scale=da_scales[e, si][:],
                    start=(si == 0),
                    stop=(si == SI - 1),
                )
                if si == SI - 1:
                    nc.scalar.activation(out=dx[e, k][:], in_=banks[e, "x", k][:], func=COPY, scale=2.0)

        def scatter(e, k):
            nc.vector.tensor_copy(win[k][:].indirect(offsets[:, e * C // 16 : (e + 1) * C // 16]), dx[e, k][:])

        permute_w2_words(0)
        for s in range(SN):
            for t in range(PACK):
                gather(0, s, t)
        permute_w2_scales()
        quantize_g(0, 0)
        for j in range(6):
            first(0, j, 0)
        for t in range(3):
            gather(1, 0, t)
        quantize_g(0, 1)
        gather(1, 0, 3)
        for j in range(4):
            derive(0, j)
        for t in range(3):
            gather(1, 1, t)
        quantize_g(1, 0)
        gather(1, 1, 3)
        second(0, 0)
        permute_w2_words(1)
        for j in range(4, 6):
            derive(0, j)
        quantize_g(1, 1)
        for j in range(6, 8):
            derive(0, j)
        for j in range(6):
            first(1, j, 0)
        for j in range(5):
            derive(1, j)
        second(0, 1)
        for j in range(5, 8):
            derive(1, j)
        second(1, 0)
        scatter(0, 0)
        second(1, 1)
        scatter(0, 1)
        for k in range(KT):
            scatter(1, k)
            nc.sync.dma_start(out[k * P : (k + 1) * P, :], win[k][:])
